import numpy as np
import ml_dtypes


def mxq(x, axis, fmt="e4m3"):
    dtype, down = {"e4m3": (ml_dtypes.float8_e4m3fn, 7), "e5m2": (ml_dtypes.float8_e5m2, 14)}[fmt]
    v = np.moveaxis(np.asarray(x, np.float32).astype(ml_dtypes.bfloat16).astype(np.float64), axis, -1)
    blocks = v.reshape(v.shape[:-1] + (-1, 32))
    amax = np.abs(blocks).max(-1, keepdims=True)
    byte = np.maximum(np.where(amax > 0, np.frexp(amax)[1] - 1 + 127, 0) - down, 1)
    scale = np.exp2(byte - 127.0)
    codes = (blocks / scale).astype(np.float32).astype(dtype).astype(np.float64)
    return np.moveaxis((codes * scale).reshape(v.shape), -1, axis)


WIDE = False


def mx_kscale(k):
    if not WIDE:
        return np.ones(k)
    levels = np.array([10, -10, 5, -5, 0])
    if k % 512:
        return np.exp2(np.random.permutation(np.resize(levels, k // 32))).repeat(32)
    a = np.empty((k // 512, 16))
    for p in range(k // 512):
        a[p, :8] = np.random.permutation(np.resize(levels, 8))
        for g in range(8):
            far = levels[np.abs(levels - a[p, g]) >= 10]
            a[p, g + 8] = far[np.random.randint(len(far))]
    return np.exp2(a.ravel()).repeat(32)


def f64(x):
    return np.asarray(x).astype(np.float64)


def striped(idx):
    return np.tile(np.asarray(idx).reshape(-1, 16).T, (8, 1)).astype(np.uint16)


def unstriped(offs):
    return offs[:16].T.reshape(-1).astype(np.int64)


E2M1 = np.array([0.0, 0.5, 1.0, 1.5, 2.0, 3.0, 4.0, 6.0, -0.0, -0.5, -1.0, -1.5, -2.0, -3.0, -4.0, -6.0])


def pack_weight(w, fmt):
    k, n = w.shape
    w = f64(np.asarray(w, np.float32).astype(ml_dtypes.bfloat16)).reshape(k // 32, 32, n)
    amax = np.abs(w).max(1)
    if fmt == "e4m3":
        byte = np.frexp(amax)[1] - 1 + 127 - 7
    else:
        mant, ex = np.frexp(amax / 6.0)
        byte = np.where(mant > 0.5, ex, ex - 1) + 127
    byte = np.clip(np.where(amax > 0, byte, 1), 1, 254)
    scaled = (w * np.exp2(127.0 - byte)[:, None, :]).reshape(k, n).astype(np.float32)
    by_word = np.ascontiguousarray(scaled.reshape(k // 512, 128, 4, n).transpose(0, 1, 3, 2))
    if fmt == "e4m3":
        words = by_word.astype(ml_dtypes.float8_e4m3fn).view(np.uint8)
    else:
        c = by_word.astype(ml_dtypes.float4_e2m1fn).view(np.uint8) & 0xF
        words = (c[..., 0::2] | (c[..., 1::2] << 4)).reshape(k // 512, 128, 2 * n)
    return np.ascontiguousarray(words), np.ascontiguousarray(byte.astype(np.uint8).reshape(k // 512, 16, n))


def unpack_weight(words, scales, fmt):
    g, _, n = scales.shape
    words = np.ascontiguousarray(words).reshape(g, 128, n, -1)
    if fmt == "e4m3":
        vals = words.view(ml_dtypes.float8_e4m3fn).astype(np.float64)
    else:
        nib = np.empty((g, 128, n, 4), np.uint8)
        nib[..., 0::2] = words & 0xF
        nib[..., 1::2] = words >> 4
        vals = E2M1[nib]
    vals = vals * np.repeat(np.exp2(scales.astype(np.float64) - 127.0), 8, axis=1)[..., None]
    return vals.transpose(0, 1, 3, 2).reshape(g * 512, n)


def sigmoid(v):
    return 1.0 / (1.0 + np.exp(-v))


K, T, J, N = 1024, 1024, 512, 512


def setup_inputs():
    n = np.random.standard_normal
    idx = np.random.permutation(T)[:J]
    idx2 = np.random.permutation(T)[:J]
    fk = mx_kscale(K)
    xqp = pack_weight(n((K, T)) / fk[:, None], "e2m1")
    wap = pack_weight(n((K, N)) * 1 / np.sqrt(K) * fk[:, None], "e2m1")
    return {
        "xq_words": xqp[0],
        "xq_scales": xqp[1],
        "wa_words": wap[0],
        "wa_scales": wap[1],
        "wb": (n((K, N)) * 1 / np.sqrt(K) * fk[:, None]).astype(np.float32),
        "gate": (1.0 * n((N, T))).astype(np.float32),
        "offs": striped(idx),
        "offs2": striped(idx2),
    }


def reference(xq_words, xq_scales, wa_words, wa_scales, wb, gate, offs, offs2):
    idx = unstriped(offs)
    idx2 = unstriped(offs2)
    xqu = unpack_weight(xq_words, xq_scales, "e2m1")
    wau = unpack_weight(wa_words, wa_scales, "e2m1")
    xqidxg = xqu[:, idx]
    p = wau.T @ xqidxg
    wbq = mxq(f64(wb), 0, "e4m3")
    xqidx2g = xqu[:, idx2]
    q = wbq.T @ xqidx2g
    pg = np.zeros((N, T))
    pg[:, idx2] = p
    qg = np.zeros((N, T))
    qg[:, idx] = q
    y = (pg + qg) * sigmoid(f64(gate))
    return y

@@ -1,0 +1,173 @@
+from contextlib import ExitStack
+
+import concourse.mybir as mybir
+
+K, T, J, N = 1024, 1024, 512, 512
+FLOPS = 2 * 2 * K * J * N
+
+F32 = mybir.dt.float32
+BF16 = mybir.dt.bfloat16
+I32 = mybir.dt.int32
+U32 = mybir.dt.uint32
+U16 = mybir.dt.uint16
+U8 = mybir.dt.uint8
+FP8X4 = mybir.dt.float8_e4m3fn_x4
+FP4X4 = mybir.dt.float4_e2m1fn_x4
+ADD = mybir.AluOpType.add
+MULT = mybir.AluOpType.mult
+SIGMOID = mybir.ActivationFunctionType.Sigmoid
+
+P = 128
+PACK = 4
+PASSES = K // (P * PACK)
+QUADS = 4
+QUAD = P // QUADS
+ROWS = 4
+TILES = N // P
+HALF = N // 2
+SHIFTED = 112
+
+
+def tile_list_experts_exchange_kernel(tc, xq_words, xq_scales, wa_words, wa_scales, wb, gate, offs, offs2, out):
+    nc = tc.nc
+    with ExitStack() as ctx:
+        keep = ctx.enter_context(tc.tile_pool(name="keep", bufs=1))
+        stage = ctx.enter_context(tc.tile_pool(name="stage", bufs=4))
+        psum = ctx.enter_context(tc.psum_pool(name="psum", bufs=1))
+
+        lists = [keep.tile([P, J // 16], U16, name=f"list{i}") for i in range(2)]
+        xs_window = keep.tile([P, T], U8, align_bytes=64)
+        wa_planes = keep.tile([P, PASSES * N], U8, align_bytes=64)
+        wa_codes = keep.tile([P, PASSES * 2 * N], U8, align_bytes=64)
+        picked_scales = [keep.tile([P, J], U8, name=f"picked_scales{i}", align_bytes=64) for i in range(2)]
+        moved_scales = [keep.tile([P, J], U8, name=f"moved_scales{i}", align_bytes=64) for i in range(2)]
+        pages = [[keep.tile([P, T], F32, name=f"page{e}{b}") for b in range(2)] for e in range(2)]
+
+        nc.vector.memset(xs_window[:].bitcast(I32), 0)
+        nc.vector.memset(wa_planes[:].bitcast(I32), 0)
+        for i in range(2):
+            nc.vector.memset(moved_scales[i][:].bitcast(I32), 0)
+        for b in range(2):
+            for e in range(2):
+                nc.vector.memset(pages[e][b][:], 0.0)
+
+        nc.sync.dma_start(lists[0][:], offs)
+        for q in range(QUADS):
+            nc.scalar.dma_start(
+                xs_window[QUAD * q : QUAD * q + PASSES * ROWS, :].bitcast(I32),
+                xq_scales[:, ROWS * q : ROWS * (q + 1), :].bitcast(I32),
+            )
+        xw_windows = []
+        for z in range(PASSES):
+            window = stage.tile([P, T], U16, name=f"xw_window{z}", tag="stage", align_bytes=64)
+            nc.sync.dma_start(window[:].bitcast(I32), xq_words[z].bitcast(I32))
+            xw_windows.append(window)
+        nc.sync.dma_start(lists[1][:], offs2)
+        nc.sync.dma_start(
+            wa_codes[:].bitcast(I32).rearrange("p (z w) -> p z w", z=PASSES),
+            wa_words.bitcast(I32).rearrange("z p w -> p z w"),
+        )
+        for q in range(QUADS):
+            nc.scalar.dma_start(
+                wa_planes[QUAD * q : QUAD * q + ROWS, :].bitcast(I32).rearrange("r (z w) -> r z w", z=PASSES),
+                wa_scales[:, ROWS * q : ROWS * (q + 1), :].bitcast(I32).rearrange("z r w -> r z w"),
+            )
+
+        wb_rows = wb.rearrange("(z p j) n -> z p j n", z=PASSES, j=PACK)
+
+        def load_wb(h, z):
+            raw = stage.tile([P, PACK, HALF], F32, name=f"wb_raw{h}{z}", tag="stage", align_bytes=64)
+            nc.sync.dma_start(raw[:], wb_rows[z][:, :, h * HALF : (h + 1) * HALF])
+            return raw
+
+        def load_gate(i):
+            raw = stage.tile([P, T], F32, name=f"gate_raw{i}", tag="stage", align_bytes=64)
+            nc.sync.dma_start(raw[:], gate[i * P : (i + 1) * P, :])
+            return raw
+
+        wb_raw = {(0, z): load_wb(0, z) for z in range(PASSES)}
+
+        picked_words = [[keep.tile([P, J], U16, name=f"picked_words{i}{z}", align_bytes=64) for z in range(PASSES)] for i in range(2)]
+        for i in range(2):
+            nc.vector.tensor_copy(picked_scales[i][:], xs_window[:].indirect(lists[i][:]))
+            nc.sync.dma_start(
+                moved_scales[i][0:SHIFTED, :].bitcast(I32),
+                picked_scales[i][ROWS : ROWS + SHIFTED, :].bitcast(I32),
+            )
+            for z in range(PASSES):
+                nc.vector.tensor_copy(picked_words[i][z][:], xw_windows[z][:].indirect(lists[i][:]))
+        x_planes = [[picked_scales[i], moved_scales[i]] for i in range(2)]
+
+        for z in range(PASSES):
+            wb_raw[(1, z)] = load_wb(1, z)
+        gate_raw = [load_gate(i) for i in range(TILES)]
+
+        grouped = [keep.tile([P, PASSES * HALF * PACK], BF16, name=f"grouped{h}", align_bytes=64) for h in range(2)]
+        wb_codes = [keep.tile([P, PASSES * HALF], U32, name=f"wb_codes{h}", align_bytes=64) for h in range(2)]
+        wb_planes = [keep.tile([P, PASSES * HALF], U8, name=f"wb_planes{h}", align_bytes=64) for h in range(2)]
+
+        def interleave(h):
+            for z in range(PASSES):
+                width = HALF * PACK
+                nc.scalar.copy(
+                    grouped[h][:, z * width : (z + 1) * width].rearrange("p (c i t) -> p c t i", i=4, t=PACK),
+                    wb_raw[(h, z)][:].rearrange("p t (c i) -> p c t i", i=4),
+                )
+
+        def quantise(h):
+            nc.vector.quantize_mx(out=wb_codes[h][:].bitcast(FP8X4), scales=wb_planes[h][:], in_=grouped[h][:])
+
+        def product(e, i):
+            acc = psum.tile([P, J], F32, name=f"acc{e}{i}")
+            for z in range(PASSES):
+                if e == 0:
+                    first = z * N + i * P
+                    codes = wa_codes[:, 2 * first : 2 * (first + P)].bitcast(FP4X4)
+                    plane = wa_planes[:, first : first + P]
+                else:
+                    h, c = divmod(i * P, HALF)
+                    first = z * HALF + c
+                    codes = wb_codes[h][:, first : first + P].bitcast(FP8X4)
+                    plane = wb_planes[h][:, first : first + P]
+                nc.tensor.matmul_mx(
+                    out=acc[:],
+                    lhsT=codes,
+                    lhsT_scale=plane,
+                    rhs=picked_words[e][z][:].bitcast(FP4X4),
+                    rhs_scale=x_planes[e][z][:],
+                    start=(z == 0),
+                    stop=(z == PASSES - 1),
+                )
+            values = keep.tile([P, J], F32, name=f"values{e}{i}")
+            nc.scalar.copy(values[:], acc[:])
+            return values
+
+        def scatter(e, i, values):
+            nc.vector.tensor_copy(pages[e][i % 2][:].indirect(lists[1 - e][:]), values[:])
+
+        interleave(0)
+        for i in range(TILES):
+            p_values = product(0, i)
+            scatter(0, i, p_values)
+            if i % 2 == 0:
+                quantise(i // 2)
+            q_values = product(1, i)
+            scatter(1, i, q_values)
+            if i == 0:
+                interleave(1)
+            sig = keep.tile([P, T], F32, name=f"sig{i}")
+            nc.scalar.activation(sig[:], gate_raw[i][:], SIGMOID)
+            total = keep.tile([P, T], F32, name=f"total{i}")
+            result = keep.tile([P, T], F32, name=f"result{i}")
+            rows = slice(i * P, (i + 1) * P)
+            if i < TILES - 1:
+                nc.gpsimd.tensor_tensor(total[:], pages[0][i % 2][:], pages[1][i % 2][:], ADD)
+                nc.gpsimd.tensor_tensor(result[:], total[:], sig[:], MULT)
+                nc.sync.dma_start(out[rows, :], result[:])
+            else:
+                halves = [slice(0, T // 2), slice(T // 2, T)]
+                for cols in halves:
+                    nc.vector.tensor_tensor(total[:, cols], pages[0][i % 2][:, cols], pages[1][i % 2][:, cols], ADD)
+                for cols in halves:
+                    nc.vector.tensor_tensor(result[:, cols], total[:, cols], sig[:, cols], MULT)
+                    nc.sync.dma_start(out[rows, cols], result[:, cols])

@@ -32,24 +32,21 @@ def tile_list_experts_exchange_kernel(tc, xq_words, xq_scales, wa_words, wa_scal
     nc = tc.nc
     with ExitStack() as ctx:
         keep = ctx.enter_context(tc.tile_pool(name="keep", bufs=1))
-        stage = ctx.enter_context(tc.tile_pool(name="stage", bufs=4))
         psum = ctx.enter_context(tc.psum_pool(name="psum", bufs=1))
 
         lists = [keep.tile([P, J // 16], U16, name=f"list{i}") for i in range(2)]
-        xs_window = keep.tile([P, T], U8, align_bytes=64)
+        xs_window = keep.tile([P, T], U8, tag="scales", align_bytes=64)
         wa_planes = keep.tile([P, PASSES * N], U8, align_bytes=64)
         wa_codes = keep.tile([P, PASSES * 2 * N], U8, align_bytes=64)
         picked_scales = [keep.tile([P, J], U8, name=f"picked_scales{i}", align_bytes=64) for i in range(2)]
-        moved_scales = [keep.tile([P, J], U8, name=f"moved_scales{i}", align_bytes=64) for i in range(2)]
-        pages = [[keep.tile([P, T], F32, name=f"page{e}{b}") for b in range(2)] for e in range(2)]
+        moved_scales = keep.tile([P, 2 * J], U8, align_bytes=64)
+        pages = {(e, 0): keep.tile([P, T], F32, name=f"page{e}0") for e in range(2)}
 
         nc.vector.memset(xs_window[:].bitcast(I32), 0)
         nc.vector.memset(wa_planes[:].bitcast(I32), 0)
-        for i in range(2):
-            nc.vector.memset(moved_scales[i][:].bitcast(I32), 0)
-        for b in range(2):
-            for e in range(2):
-                nc.vector.memset(pages[e][b][:], 0.0)
+        nc.vector.memset(moved_scales[:].bitcast(I32), 0)
+        for e in range(2):
+            nc.vector.memset(pages[(e, 0)][:], 0.0)
 
         nc.sync.dma_start(lists[0][:], offs)
         for q in range(QUADS):
@@ -59,7 +56,7 @@ def tile_list_experts_exchange_kernel(tc, xq_words, xq_scales, wa_words, wa_scal
             )
         xw_windows = []
         for z in range(PASSES):
-            window = stage.tile([P, T], U16, name=f"xw_window{z}", tag="stage", align_bytes=64)
+            window = keep.tile([P, T], U16, name=f"xw_window{z}", tag=f"words{z}", align_bytes=64)
             nc.sync.dma_start(window[:].bitcast(I32), xq_words[z].bitcast(I32))
             xw_windows.append(window)
         nc.sync.dma_start(lists[1][:], offs2)
@@ -74,51 +71,48 @@ def tile_list_experts_exchange_kernel(tc, xq_words, xq_scales, wa_words, wa_scal
             )
 
         wb_rows = wb.rearrange("(z p j) n -> z p j n", z=PASSES, j=PACK)
+        wb_raw = {}
+        for z in range(PASSES):
+            raw = keep.tile([P, PACK, HALF], F32, name=f"wb_raw0{z}", tag=f"raw{z}", align_bytes=64)
+            nc.sync.dma_start(raw[:], wb_rows[z][:, :, 0:HALF])
+            wb_raw[(0, z)] = raw[:]
 
-        def load_wb(h, z):
-            raw = stage.tile([P, PACK, HALF], F32, name=f"wb_raw{h}{z}", tag="stage", align_bytes=64)
-            nc.sync.dma_start(raw[:], wb_rows[z][:, :, h * HALF : (h + 1) * HALF])
-            return raw
-
-        def load_gate(i):
-            raw = stage.tile([P, T], F32, name=f"gate_raw{i}", tag="stage", align_bytes=64)
-            nc.sync.dma_start(raw[:], gate[i * P : (i + 1) * P, :])
-            return raw
-
-        wb_raw = {(0, z): load_wb(0, z) for z in range(PASSES)}
-
-        picked_words = [[keep.tile([P, J], U16, name=f"picked_words{i}{z}", align_bytes=64) for z in range(PASSES)] for i in range(2)]
+        first_words = keep.tile([P, J], U16, align_bytes=64)
+        nc.vector.tensor_copy(first_words[:], xw_windows[0][:].indirect(lists[0][:]))
         for i in range(2):
             nc.vector.tensor_copy(picked_scales[i][:], xs_window[:].indirect(lists[i][:]))
             nc.sync.dma_start(
-                moved_scales[i][0:SHIFTED, :].bitcast(I32),
+                moved_scales[0:SHIFTED, i * J : (i + 1) * J].bitcast(I32),
                 picked_scales[i][ROWS : ROWS + SHIFTED, :].bitcast(I32),
             )
-            for z in range(PASSES):
-                nc.vector.tensor_copy(picked_words[i][z][:], xw_windows[z][:].indirect(lists[i][:]))
-        x_planes = [[picked_scales[i], moved_scales[i]] for i in range(2)]
+        later_words = keep.tile([P, 3 * J], U16, tag="scales", align_bytes=64)
+        picked_words = [[first_words[:], later_words[:, 0:J]], [later_words[:, J : 2 * J], later_words[:, 2 * J : 3 * J]]]
+        for i, z in ((0, 1), (1, 0), (1, 1)):
+            nc.vector.tensor_copy(picked_words[i][z], xw_windows[z][:].indirect(lists[i][:]))
+        x_planes = [[picked_scales[i][:], moved_scales[:, i * J : (i + 1) * J]] for i in range(2)]
 
-        for z in range(PASSES):
-            wb_raw[(1, z)] = load_wb(1, z)
-        gate_raw = [load_gate(i) for i in range(TILES)]
+        for e in range(2):
+            pages[(e, 1)] = keep.tile([P, T], F32, name=f"page{e}1", tag=f"words{e}", align_bytes=64)
+            nc.gpsimd.memset(pages[(e, 1)][:], 0.0)
 
-        grouped = [keep.tile([P, PASSES * HALF * PACK], BF16, name=f"grouped{h}", align_bytes=64) for h in range(2)]
         wb_codes = [keep.tile([P, PASSES * HALF], U32, name=f"wb_codes{h}", align_bytes=64) for h in range(2)]
         wb_planes = [keep.tile([P, PASSES * HALF], U8, name=f"wb_planes{h}", align_bytes=64) for h in range(2)]
 
-        def interleave(h):
-            for z in range(PASSES):
-                width = HALF * PACK
-                nc.scalar.copy(
-                    grouped[h][:, z * width : (z + 1) * width].rearrange("p (c i t) -> p c t i", i=4, t=PACK),
-                    wb_raw[(h, z)][:].rearrange("p t (c i) -> p c t i", i=4),
-                )
-
         def quantise(h):
-            nc.vector.quantize_mx(out=wb_codes[h][:].bitcast(FP8X4), scales=wb_planes[h][:], in_=grouped[h][:])
+            grouped = keep.tile([P, PASSES * HALF * PACK], BF16, name=f"grouped{h}", tag=f"grouped{h}", align_bytes=64)
+            width = HALF * PACK
+            for z in range(PASSES):
+                nc.scalar.copy(
+                    grouped[:, z * width : (z + 1) * width].rearrange("p (c i t) -> p c t i", i=4, t=PACK),
+                    wb_raw[(h, z)].rearrange("p t (c i) -> p c t i", i=4),
+                )
+            nc.vector.quantize_mx(out=wb_codes[h][:].bitcast(FP8X4), scales=wb_planes[h][:], in_=grouped[:])
+
+        banks = {(0, 3): "acc12"}
+        homes = {(0, 0): "raw1", (0, 2): "raw0"}
 
         def product(e, i):
-            acc = psum.tile([P, J], F32, name=f"acc{e}{i}")
+            acc = psum.tile([P, J], F32, name=f"acc{e}{i}", tag=banks.get((e, i), f"acc{e}{i}"))
             for z in range(PASSES):
                 if e == 0:
                     first = z * N + i * P
@@ -133,41 +127,50 @@ def tile_list_experts_exchange_kernel(tc, xq_words, xq_scales, wa_words, wa_scal
                     out=acc[:],
                     lhsT=codes,
                     lhsT_scale=plane,
-                    rhs=picked_words[e][z][:].bitcast(FP4X4),
-                    rhs_scale=x_planes[e][z][:],
+                    rhs=picked_words[e][z].bitcast(FP4X4),
+                    rhs_scale=x_planes[e][z],
                     start=(z == 0),
                     stop=(z == PASSES - 1),
                 )
-            values = keep.tile([P, J], F32, name=f"values{e}{i}")
+            values = keep.tile([P, J], F32, name=f"values{e}{i}", tag=homes.get((e, i), f"values{e}{i}"), align_bytes=64)
             nc.scalar.copy(values[:], acc[:])
-            return values
+            nc.vector.tensor_copy(pages[(e, i % 2)][:].indirect(lists[1 - e][:]), values[:])
 
-        def scatter(e, i, values):
-            nc.vector.tensor_copy(pages[e][i % 2][:].indirect(lists[1 - e][:]), values[:])
-
-        interleave(0)
-        for i in range(TILES):
-            p_values = product(0, i)
-            scatter(0, i, p_values)
-            if i % 2 == 0:
-                quantise(i // 2)
-            q_values = product(1, i)
-            scatter(1, i, q_values)
-            if i == 0:
-                interleave(1)
+        def finish(i):
+            rows = slice(i * P, (i + 1) * P)
             sig = keep.tile([P, T], F32, name=f"sig{i}")
-            nc.scalar.activation(sig[:], gate_raw[i][:], SIGMOID)
+            nc.scalar.activation(sig[:], gates[:, i], SIGMOID)
             total = keep.tile([P, T], F32, name=f"total{i}")
             result = keep.tile([P, T], F32, name=f"result{i}")
-            rows = slice(i * P, (i + 1) * P)
             if i < TILES - 1:
-                nc.gpsimd.tensor_tensor(total[:], pages[0][i % 2][:], pages[1][i % 2][:], ADD)
+                nc.gpsimd.tensor_tensor(total[:], pages[(0, i % 2)][:], pages[(1, i % 2)][:], ADD)
                 nc.gpsimd.tensor_tensor(result[:], total[:], sig[:], MULT)
                 nc.sync.dma_start(out[rows, :], result[:])
             else:
                 halves = [slice(0, T // 2), slice(T // 2, T)]
                 for cols in halves:
-                    nc.vector.tensor_tensor(total[:, cols], pages[0][i % 2][:, cols], pages[1][i % 2][:, cols], ADD)
+                    nc.vector.tensor_tensor(total[:, cols], pages[(0, i % 2)][:, cols], pages[(1, i % 2)][:, cols], ADD)
                 for cols in halves:
                     nc.vector.tensor_tensor(result[:, cols], total[:, cols], sig[:, cols], MULT)
                     nc.sync.dma_start(out[rows, cols], result[:, cols])
+
+        quantise(0)
+        second = keep.tile([P, PASSES, PACK, HALF], F32, name="wb_raw1", tag="raw0", align_bytes=64)
+        for z in range(PASSES):
+            nc.sync.dma_start(second[:, z], wb_rows[z][:, :, HALF:N])
+            wb_raw[(1, z)] = second[:, z]
+        gates = keep.tile([P, TILES, T], F32, tag="grouped0", align_bytes=64)
+        for i in range(TILES):
+            nc.sync.dma_start(gates[:, i], gate[i * P : (i + 1) * P, :])
+        for i in range(2):
+            product(0, i)
+            product(1, i)
+        quantise(1)
+        finish(0)
+        finish(1)
+        product(0, 2)
+        product(1, 2)
+        finish(2)
+        product(0, 3)
+        product(1, 3)
+        finish(3)

@@ -91,25 +91,24 @@ def tile_list_experts_exchange_kernel(tc, xq_words, xq_scales, wa_words, wa_scal
             nc.vector.tensor_copy(picked_words[i][z], xw_windows[z][:].indirect(lists[i][:]))
         x_planes = [[picked_scales[i][:], moved_scales[:, i * J : (i + 1) * J]] for i in range(2)]
 
-        for e in range(2):
-            pages[(e, 1)] = keep.tile([P, T], F32, name=f"page{e}1", tag=f"words{e}", align_bytes=64)
-            nc.gpsimd.memset(pages[(e, 1)][:], 0.0)
-
         wb_codes = [keep.tile([P, PASSES * HALF], U32, name=f"wb_codes{h}", align_bytes=64) for h in range(2)]
         wb_planes = [keep.tile([P, PASSES * HALF], U8, name=f"wb_planes{h}", align_bytes=64) for h in range(2)]
 
         def quantise(h):
-            grouped = keep.tile([P, PASSES * HALF * PACK], BF16, name=f"grouped{h}", tag=f"grouped{h}", align_bytes=64)
             width = HALF * PACK
-            for z in range(PASSES):
-                nc.scalar.copy(
-                    grouped[:, z * width : (z + 1) * width].rearrange("p (c i t) -> p c t i", i=4, t=PACK),
-                    wb_raw[(h, z)].rearrange("p t (c i) -> p c t i", i=4),
-                )
-            nc.vector.quantize_mx(out=wb_codes[h][:].bitcast(FP8X4), scales=wb_planes[h][:], in_=grouped[:])
+            for passes in ([[0], [1]] if h == 0 else [[0, 1]]):
+                first = passes[0]
+                grouped = keep.tile([P, len(passes) * width], BF16, name=f"grouped{h}{first}", tag=f"grouped{h}{first}", align_bytes=64)
+                for z in passes:
+                    nc.scalar.copy(
+                        grouped[:, (z - first) * width : (z - first + 1) * width].rearrange("p (c i t) -> p c t i", i=4, t=PACK),
+                        wb_raw[(h, z)].rearrange("p t (c i) -> p c t i", i=4),
+                    )
+                cols = slice(first * HALF, (passes[-1] + 1) * HALF)
+                nc.vector.quantize_mx(out=wb_codes[h][:, cols].bitcast(FP8X4), scales=wb_planes[h][:, cols], in_=grouped[:])
 
-        banks = {(0, 3): "acc12"}
-        homes = {(0, 0): "raw1", (0, 2): "raw0"}
+        banks = {(0, 1): "acc10"}
+        homes = {(0, 0): "raw1", (0, 1): "grouped00", (1, 1): "grouped10"}
 
         def product(e, i):
             acc = psum.tile([P, J], F32, name=f"acc{e}{i}", tag=banks.get((e, i), f"acc{e}{i}"))
@@ -140,7 +139,7 @@ def tile_list_experts_exchange_kernel(tc, xq_words, xq_scales, wa_words, wa_scal
             rows = slice(i * P, (i + 1) * P)
             sig = keep.tile([P, T], F32, name=f"sig{i}")
             nc.scalar.activation(sig[:], gates[:, i], SIGMOID)
-            total = keep.tile([P, T], F32, name=f"total{i}")
+            total = keep.tile([P, T], F32, name=f"total{i}", tag=f"total{min(i, TILES - 2)}")
             result = keep.tile([P, T], F32, name=f"result{i}")
             if i < TILES - 1:
                 nc.gpsimd.tensor_tensor(total[:], pages[(0, i % 2)][:], pages[(1, i % 2)][:], ADD)
@@ -155,17 +154,21 @@ def tile_list_experts_exchange_kernel(tc, xq_words, xq_scales, wa_words, wa_scal
                     nc.sync.dma_start(out[rows, cols], result[:, cols])
 
         quantise(0)
-        second = keep.tile([P, PASSES, PACK, HALF], F32, name="wb_raw1", tag="raw0", align_bytes=64)
-        for z in range(PASSES):
-            nc.sync.dma_start(second[:, z], wb_rows[z][:, :, HALF:N])
-            wb_raw[(1, z)] = second[:, z]
-        gates = keep.tile([P, TILES, T], F32, tag="grouped0", align_bytes=64)
+        for z, home in enumerate(("raw0", "grouped00")):
+            raw = keep.tile([P, PACK, HALF], F32, name=f"wb_raw1{z}", tag=home, align_bytes=64)
+            nc.sync.dma_start(raw[:], wb_rows[z][:, :, HALF:N])
+            wb_raw[(1, z)] = raw[:]
+        product(0, 0)
+        for e, home in enumerate(("grouped01", "raw1")):
+            pages[(e, 1)] = keep.tile([P, T], F32, name=f"page{e}1", tag=home, align_bytes=64)
+            nc.gpsimd.memset(pages[(e, 1)][:], 0.0)
+        product(1, 0)
+        quantise(1)
+        gates = keep.tile([P, TILES, T], F32, tag="raw0", align_bytes=64)
         for i in range(TILES):
             nc.sync.dma_start(gates[:, i], gate[i * P : (i + 1) * P, :])
-        for i in range(2):
-            product(0, i)
-            product(1, i)
-        quantise(1)
+        product(0, 1)
+        product(1, 1)
         finish(0)
         finish(1)
         product(0, 2)

from contextlib import ExitStack

import concourse.mybir as mybir

K, T, J, N = 1024, 1024, 512, 512
FLOPS = 2 * 2 * K * J * N

F32 = mybir.dt.float32
BF16 = mybir.dt.bfloat16
I32 = mybir.dt.int32
U32 = mybir.dt.uint32
U16 = mybir.dt.uint16
U8 = mybir.dt.uint8
FP8X4 = mybir.dt.float8_e4m3fn_x4
FP4X4 = mybir.dt.float4_e2m1fn_x4
ADD = mybir.AluOpType.add
MULT = mybir.AluOpType.mult
SIGMOID = mybir.ActivationFunctionType.Sigmoid

P = 128
PACK = 4
PASSES = K // (P * PACK)
QUADS = 4
QUAD = P // QUADS
ROWS = 4
TILES = N // P
HALF = N // 2
SHIFTED = 112


def tile_list_experts_exchange_kernel(tc, xq_words, xq_scales, wa_words, wa_scales, wb, gate, offs, offs2, out):
    nc = tc.nc
    with ExitStack() as ctx:
        keep = ctx.enter_context(tc.tile_pool(name="keep", bufs=1))
        psum = ctx.enter_context(tc.psum_pool(name="psum", bufs=1))

        lists = [keep.tile([P, J // 16], U16, name=f"list{i}") for i in range(2)]
        xs_window = keep.tile([P, T], U8, tag="scales", align_bytes=64)
        wa_planes = keep.tile([P, PASSES * N], U8, align_bytes=64)
        wa_codes = keep.tile([P, PASSES * 2 * N], U8, align_bytes=64)
        picked_scales = [keep.tile([P, J], U8, name=f"picked_scales{i}", align_bytes=64) for i in range(2)]
        moved_scales = keep.tile([P, 2 * J], U8, align_bytes=64)
        pages = {(e, 0): keep.tile([P, T], F32, name=f"page{e}0") for e in range(2)}

        nc.vector.memset(xs_window[:].bitcast(I32), 0)
        nc.vector.memset(wa_planes[:].bitcast(I32), 0)
        nc.vector.memset(moved_scales[:].bitcast(I32), 0)
        for e in range(2):
            nc.vector.memset(pages[(e, 0)][:], 0.0)

        nc.sync.dma_start(lists[0][:], offs)
        for q in range(QUADS):
            nc.scalar.dma_start(
                xs_window[QUAD * q : QUAD * q + PASSES * ROWS, :].bitcast(I32),
                xq_scales[:, ROWS * q : ROWS * (q + 1), :].bitcast(I32),
            )
        xw_windows = []
        for z in range(PASSES):
            window = keep.tile([P, T], U16, name=f"xw_window{z}", tag=f"words{z}", align_bytes=64)
            nc.sync.dma_start(window[:].bitcast(I32), xq_words[z].bitcast(I32))
            xw_windows.append(window)
        nc.sync.dma_start(lists[1][:], offs2)
        nc.sync.dma_start(
            wa_codes[:].bitcast(I32).rearrange("p (z w) -> p z w", z=PASSES),
            wa_words.bitcast(I32).rearrange("z p w -> p z w"),
        )
        for q in range(QUADS):
            nc.scalar.dma_start(
                wa_planes[QUAD * q : QUAD * q + ROWS, :].bitcast(I32).rearrange("r (z w) -> r z w", z=PASSES),
                wa_scales[:, ROWS * q : ROWS * (q + 1), :].bitcast(I32).rearrange("z r w -> r z w"),
            )

        wb_rows = wb.rearrange("(z p j) n -> z p j n", z=PASSES, j=PACK)
        wb_raw = {}
        for z in range(PASSES):
            raw = keep.tile([P, PACK, HALF], F32, name=f"wb_raw0{z}", tag=f"raw{z}", align_bytes=64)
            nc.sync.dma_start(raw[:], wb_rows[z][:, :, 0:HALF])
            wb_raw[(0, z)] = raw[:]

        first_words = keep.tile([P, J], U16, align_bytes=64)
        nc.vector.tensor_copy(first_words[:], xw_windows[0][:].indirect(lists[0][:]))
        for i in range(2):
            nc.vector.tensor_copy(picked_scales[i][:], xs_window[:].indirect(lists[i][:]))
            nc.sync.dma_start(
                moved_scales[0:SHIFTED, i * J : (i + 1) * J].bitcast(I32),
                picked_scales[i][ROWS : ROWS + SHIFTED, :].bitcast(I32),
            )
        later_words = keep.tile([P, 3 * J], U16, tag="scales", align_bytes=64)
        picked_words = [[first_words[:], later_words[:, 0:J]], [later_words[:, J : 2 * J], later_words[:, 2 * J : 3 * J]]]
        for i, z in ((0, 1), (1, 0), (1, 1)):
            nc.vector.tensor_copy(picked_words[i][z], xw_windows[z][:].indirect(lists[i][:]))
        x_planes = [[picked_scales[i][:], moved_scales[:, i * J : (i + 1) * J]] for i in range(2)]

        wb_codes = [keep.tile([P, PASSES * HALF], U32, name=f"wb_codes{h}", align_bytes=64) for h in range(2)]
        wb_planes = [keep.tile([P, PASSES * HALF], U8, name=f"wb_planes{h}", align_bytes=64) for h in range(2)]

        def quantise(h):
            width = HALF * PACK
            for passes in ([[0], [1]] if h == 0 else [[0, 1]]):
                first = passes[0]
                grouped = keep.tile([P, len(passes) * width], BF16, name=f"grouped{h}{first}", tag=f"grouped{h}{first}", align_bytes=64)
                for z in passes:
                    nc.scalar.copy(
                        grouped[:, (z - first) * width : (z - first + 1) * width].rearrange("p (c i t) -> p c t i", i=4, t=PACK),
                        wb_raw[(h, z)].rearrange("p t (c i) -> p c t i", i=4),
                    )
                cols = slice(first * HALF, (passes[-1] + 1) * HALF)
                nc.vector.quantize_mx(out=wb_codes[h][:, cols].bitcast(FP8X4), scales=wb_planes[h][:, cols], in_=grouped[:])

        banks = {(0, 1): "acc10"}
        homes = {(0, 0): "raw1", (0, 1): "grouped00", (1, 1): "grouped10"}

        def product(e, i):
            acc = psum.tile([P, J], F32, name=f"acc{e}{i}", tag=banks.get((e, i), f"acc{e}{i}"))
            for z in range(PASSES):
                if e == 0:
                    first = z * N + i * P
                    codes = wa_codes[:, 2 * first : 2 * (first + P)].bitcast(FP4X4)
                    plane = wa_planes[:, first : first + P]
                else:
                    h, c = divmod(i * P, HALF)
                    first = z * HALF + c
                    codes = wb_codes[h][:, first : first + P].bitcast(FP8X4)
                    plane = wb_planes[h][:, first : first + P]
                nc.tensor.matmul_mx(
                    out=acc[:],
                    lhsT=codes,
                    lhsT_scale=plane,
                    rhs=picked_words[e][z].bitcast(FP4X4),
                    rhs_scale=x_planes[e][z],
                    start=(z == 0),
                    stop=(z == PASSES - 1),
                )
            values = keep.tile([P, J], F32, name=f"values{e}{i}", tag=homes.get((e, i), f"values{e}{i}"), align_bytes=64)
            nc.scalar.copy(values[:], acc[:])
            nc.vector.tensor_copy(pages[(e, i % 2)][:].indirect(lists[1 - e][:]), values[:])

        def finish(i):
            rows = slice(i * P, (i + 1) * P)
            sig = keep.tile([P, T], F32, name=f"sig{i}")
            nc.scalar.activation(sig[:], gates[:, i], SIGMOID)
            total = keep.tile([P, T], F32, name=f"total{i}", tag=f"total{min(i, TILES - 2)}")
            result = keep.tile([P, T], F32, name=f"result{i}")
            if i < TILES - 1:
                nc.gpsimd.tensor_tensor(total[:], pages[(0, i % 2)][:], pages[(1, i % 2)][:], ADD)
                nc.gpsimd.tensor_tensor(result[:], total[:], sig[:], MULT)
                nc.sync.dma_start(out[rows, :], result[:])
            else:
                halves = [slice(0, T // 2), slice(T // 2, T)]
                for cols in halves:
                    nc.vector.tensor_tensor(total[:, cols], pages[(0, i % 2)][:, cols], pages[(1, i % 2)][:, cols], ADD)
                for cols in halves:
                    nc.vector.tensor_tensor(result[:, cols], total[:, cols], sig[:, cols], MULT)
                    nc.sync.dma_start(out[rows, cols], result[:, cols])

        quantise(0)
        for z, home in enumerate(("raw0", "grouped00")):
            raw = keep.tile([P, PACK, HALF], F32, name=f"wb_raw1{z}", tag=home, align_bytes=64)
            nc.sync.dma_start(raw[:], wb_rows[z][:, :, HALF:N])
            wb_raw[(1, z)] = raw[:]
        product(0, 0)
        for e, home in enumerate(("grouped01", "raw1")):
            pages[(e, 1)] = keep.tile([P, T], F32, name=f"page{e}1", tag=home, align_bytes=64)
            nc.gpsimd.memset(pages[(e, 1)][:], 0.0)
        product(1, 0)
        quantise(1)
        gates = keep.tile([P, TILES, T], F32, tag="raw0", align_bytes=64)
        for i in range(TILES):
            nc.sync.dma_start(gates[:, i], gate[i * P : (i + 1) * P, :])
        product(0, 1)
        product(1, 1)
        finish(0)
        finish(1)
        product(0, 2)
        product(1, 2)
        finish(2)
        product(0, 3)
        product(1, 3)
        finish(3)
